import numpy as np, ml_dtypes
CORES = [16,17,18,19,32,33,34,35]
N = 8
import mx_ref
BF = ml_dtypes.bfloat16
def pick(q, e):
    c = np.concatenate([q[0].reshape(128, -1, 4), np.zeros((128, 1, 4), np.uint8)], axis=1); s = np.concatenate([q[1], np.ones((16, 1), np.uint8)], axis=1)
    return (np.ascontiguousarray(c[:, e].reshape(128, -1)), np.ascontiguousarray(s[:, e]))
def join(*qs):
    return (np.concatenate([q[0] for q in qs], axis=1), np.concatenate([q[1] for q in qs], axis=1))
def put(q, e, v):
    c, s = q[0].reshape(128, -1, 4).copy(), q[1].copy(); c[:, e] = v[0].reshape(128, -1, 4); s[:, e] = v[1]
    return (c.reshape(128, -1), s)
def pk(c, s):
    return (np.ascontiguousarray(c), mx_ref.live(s))
def emit(q):
    return q[0], q[1]
def cut(t, i, w=512):
    return t[:, w * i:w * i + w]
def tile(rs):
    return np.stack(rs, axis=2).reshape(128, -1).astype(BF)
def f(rng, *shape):
    return mx_ref.flush((rng.standard_normal(shape, dtype=np.float32) * np.exp2(rng.integers(-2, 3, shape[:-1] + (1,)))).astype(BF))
def wide(rng, *shape, cols=0):
    v = rng.standard_normal(shape, dtype=np.float32) * np.exp2(rng.integers(-12, 13, shape)).astype(np.float32)
    if cols: v *= np.repeat(np.exp2(rng.integers(-cols, cols + 1, shape[:-2] + (1, shape[-1] // 4))) * (rng.random(shape[:-2] + (1, shape[-1] // 4)) > 0.0625), 4, axis=-1).astype(np.float32)
    return mx_ref.flush(v.astype(BF))
T, L, CAPP = 128, 3, 48
def game(x, u, w):
    S = [mx_ref.quantize(np.ascontiguousarray(x[r])) for r in range(N)]
    qu = [mx_ref.quantize(np.ascontiguousarray(u[r])) for r in range(N)]
    at, ks, made = np.arange(N * T).reshape(N, T), np.zeros((N, 1, L), np.float32), []
    for b in range(L):
        want = [np.flatnonzero(mx_ref.matmul(qu[r], S[r])[b] + np.float32(0) < 0) for r in range(N)]
        new, now = [], at.copy()
        for r in range(N):
            p = r ^ (1 << b)
            k = min(len(want[r]), len(want[p]), CAPP)
            to, of = want[r][:k], want[p][:k]
            c = pick(S[p], np.concatenate([of, np.full(CAPP - k, -1)]))
            t = tile([np.float32(0.0625) * mx_ref.matmul(mx_ref.quantize(np.ascontiguousarray(cut(w[r], 4 * b + i))), c) for i in range(4)])
            made.append(t)
            new.append(put(S[r], to, pick(mx_ref.quantize(t), np.arange(k))))
            now[r, to] = at[p, of]
            ks[r, 0, b] = k
        S, at = new, now
    return S, at, ks, made
def fit(t, low, high):
    a = np.abs(t.astype(np.float32))
    return bool((np.isfinite(a) & ((a == 0) | (a >= low) & (a <= high))).all())
def blocks(t):
    return np.abs(t.astype(np.float32)).reshape(16, 8, -1, 4).max(axis=(1, 3))
def plain(rng):
    u = np.array(f(rng, N, 128, 512))
    u[:, :, 4 * L:] = 0
    a = np.exp2(rng.integers(-2, 3, (N, 128, 1, 1)))
    x, lean = rng.standard_normal((N, 128, T, 4)), 2.5 * rng.random((N, L)) - 1
    for b in range(L):
        h = a * u[:, :, None, 4 * b:4 * b + 4].astype(np.float64)
        x += lean[:, b, None, None, None] * h * np.sum(h * h, axis=(1, 2, 3), keepdims=True) ** -0.5
    x = mx_ref.flush((a * x).reshape(N, 128, 4 * T).astype(np.float32).astype(BF))
    return {"x": x, "u": u, "w": f(rng, N, 128, 2048 * L), "v": f(rng, N, 128, 512)}
def aim(x, u, wish):
    x = x.reshape(N, 128, T, 4).astype(np.float32)
    for r in range(N):
        s = mx_ref.matmul(mx_ref.quantize(np.ascontiguousarray(u[r])), mx_ref.quantize(np.ascontiguousarray(x[r].reshape(128, 4 * T).astype(BF))))[0]
        x[r][:, s == 0] = u[r][:, None, :4].astype(np.float32)
        x[r][:, (s < 0) != wish[r]] *= -1
    return (x + np.float32(0)).reshape(N, 128, 4 * T).astype(BF)
def some(rng, n):
    return np.stack([rng.permutation(T) < n[r] for r in range(N)])
def setup_inputs(rng):
    return plain(rng)
def setup_inputs_many(rng):
    d = plain(rng)
    n = rng.integers(CAPP + 1, T + 1, N)
    j = 2 * int(rng.integers(0, N // 2))
    n[j:j + 2] = CAPP
    d["x"] = aim(d["x"], d["u"], some(rng, n))
    return d
def setup_inputs_none(rng):
    d = plain(rng)
    wish = some(rng, rng.integers(T // 4, T + 1, N))
    i, j = 2 * rng.permutation(N // 2)[:2] + rng.integers(0, 2, 2)
    wish[i] = False
    wish[i ^ 1] = True
    wish[j] = np.arange(T) == T - 1
    d["u"][int(rng.integers(0, N)), :, 4:8] = 0
    d["x"] = aim(d["x"], d["u"], wish)
    return d
def setup_inputs_zero(rng):
    d = plain(rng)
    d["u"][:, 64:, :4] = 0
    x = np.array(d["x"]).reshape(N, 128, T, 4)
    for r in range(N):
        e = rng.permutation(T)
        x[r][:, e[:T // 8]] = 0
        x[r][:64, e[T // 8:3 * T // 8]] = 0
    d["x"] = x.reshape(N, 128, 4 * T)
    return d
def setup_inputs_turn(rng):
    d = plain(rng)
    d["x"] = aim(d["x"], d["u"], some(rng, np.full(N, T // 2)))
    m, e = np.zeros((128, L, 4, 128, 4), np.float32), np.arange(128)
    for b in range(L):
        for i in range(4): m[e, b, i, e, i] = -16
    d["w"] = mx_ref.flush((m.reshape(128, 2048 * L) + d["w"].astype(np.float32) * np.float32(2.0 ** -6)).astype(BF))
    return d
def setup_inputs_spread(rng):
    d = plain(rng)
    u = np.array(wide(rng, N, 128, 512))
    u[:, :, 4 * L:] = 0
    return {**d, "x": wide(rng, N, 128, 4 * T, cols=6), "u": u, "v": wide(rng, N, 128, 512)}
def check_inputs(d):
    b = []
    for k in ("x", "u", "w", "v"):
        if not fit(d[k], 2.0 ** -30, 2.0 ** 30): b.append("a value of " + k)
    if (d["u"][:, :, 4 * L:].astype(np.float32) != 0).any(): b.append("u has numbers behind its first L columns")
    if not b:
        try:
            made = game(d["x"], d["u"], d["w"])[3]
            good, even = all(fit(t, 2.0 ** -60, 2.0 ** 60) for t in made), all(fit(blocks(t), 2.0 ** -30, 2.0 ** 30) for t in made)
        except Exception: good = even = False
        if not good: b.append("a number that an expert gives")
        if not even: b.append("the largest number of a block that an expert gives")
    return b
def reference(x, u, w, v):
    S, at, ks, made = game(x, u, w)
    oc, osc = np.zeros((N, 128, 4 * T), np.uint8), np.zeros((N, 16, T), np.uint8)
    y = np.zeros((N, 128, T), np.float32)
    for r in range(N):
        oc[r], osc[r] = emit(S[r])
        y[r] = mx_ref.matmul(mx_ref.quantize(np.ascontiguousarray(v[r])), S[r])
    return {"oc": oc, "osc": osc, "ids": at.reshape(N, 1, T).astype(np.float32), "ks": ks, "y": y}

@@ -1,0 +1,344 @@
+from concourse.bass import DstId, RemoteDMATransfer
+from concourse.mybir import dt, AluOpType, AxisListType, ActivationFunctionType
+
+L, CAPP, NP = 3, 48, 128
+WIN = NP + CAPP
+A = AluOpType
+F = ActivationFunctionType
+
+SCRATCH = {}
+
+
+def _mx(name, n):
+    SCRATCH["c" + name] = ("sbuf", [128, n], "float8_e4m3fn_x4")
+    SCRATCH["s" + name] = ("sbuf", [128, n], "uint8")
+
+
+def _sb(name, n, dtype="float32"):
+    SCRATCH[name] = ("sbuf", [128, n], dtype)
+
+
+for _b in range(L):
+    _mx("A%d" % _b, 128)
+    _mx("M%d" % _b, WIN)
+    _mx("X%d" % _b, WIN)
+    _mx("G%d" % _b, 128)
+    _mx("W%d" % _b, 512)
+    _sb("wt%d" % _b, 2048, "bfloat16")
+    _sb("gt%d" % _b, 512, "bfloat16")
+    _sb("ht%d" % _b, 512, "bfloat16")
+    _sb("wa%d" % _b, 128, "bfloat16")
+    _sb("cc%d" % _b, 128, "bfloat16")
+    _sb("wd%d" % _b, 128, "bfloat16")
+    _sb("yd%d" % _b, 128, "bfloat16")
+    _sb("dd%d" % _b, 128, "bfloat16")
+    _sb("jk%d" % _b, 384, "bfloat16")
+    _sb("su%d" % _b, 4)
+    _sb("sm%d" % _b, 64)
+    _sb("zz%d" % _b, 4, "uint16")
+    _sb("lo%d" % _b, 4, "uint16")
+    _sb("ml%d" % _b, 8, "uint16")
+    _sb("lz%d" % _b, 4, "uint16")
+    _sb("im%d" % _b, WIN)
+    _sb("iw%d" % _b, WIN)
+_mx("A3", 128)
+_mx("P0", 128)
+_mx("P1", 128)
+_mx("R", WIN)
+_mx("P2", 128)
+_mx("V", 128)
+_sb("xt", 512, "bfloat16")
+_sb("ut", 4 * L, "bfloat16")
+_sb("vt", 512, "bfloat16")
+_sb("zb", 128, "bfloat16")
+_sb("ia", 128, "int32")
+_sb("ib", 128, "int32")
+_sb("iq", 8, "int32")
+_sb("ir", 8, "int32")
+_sb("ic", 8)
+_sb("pj", 24)
+_sb("th", 128)
+_sb("r0", 128, "bfloat16")
+_sb("rm", 128, "bfloat16")
+_sb("cw", WIN)
+_sb("kj", CAPP * L)
+_sb("it", 256)
+_sb("pa", 8)
+_sb("px", 4, "uint16")
+_sb("pl", 4, "uint16")
+_sb("qx", 4, "uint16")
+_sb("ql", 4, "uint16")
+_sb("mx1", 4, "uint16")
+_sb("mxl", 4, "uint16")
+_sb("pm", 8, "uint16")
+_sb("ui", 16, "int32")
+_sb("uj", 16, "int32")
+_sb("un", 8)
+_sb("ex", 256)
+_sb("idf", 128)
+_sb("kk", 12)
+_sb("yt", 128)
+SCRATCH["pe"] = ("psum", [128, 2048], "float32")
+SCRATCH["ps"] = ("psum", [128, 512], "float32")
+SCRATCH["py"] = ("psum", [128, 512], "float32")
+
+SEMAPHORES = (["vs", "ss", "ts", "gs", "gi", "sent", "dx", "du", "dv", "out"]
+              + ["dw0%d" % i for i in range(4)] + ["dw%d%d" % (b, i) for b in (1, 2) for i in range(2)]
+              + ["ap0", "ap1", "ar0", "ar1", "az0", "az1", "az2", "ai1", "ai2", "aml"])
+
+
+def rank_program(g, core, T, topo):
+    rank = T.rank_of(core)
+    if rank is None:
+        return
+    peers = [T.cores[rank ^ (1 << b)] for b in range(L)]
+    queue = {"v": g.vector, "s": g.scalar, "t": g.tensor, "g": g, "y": g.sync}
+    total, known = {}, {q: {} for q in queue}
+
+    def need(q, deps):
+        for d in deps:
+            if d is None:
+                continue
+            s, n = d
+            if known[q].get(s, 0) < n:
+                queue[q].wait_ge(T.sem[s], n)
+                known[q][s] = n
+
+    def did(instr, s, n):
+        instr.then_inc(T.sem[s], n)
+        total[s] = total.get(s, 0) + n
+        return (s, total[s])
+
+    def V(call, *deps):
+        need("v", deps)
+        return did(call(g.vector), "vs", 1)
+
+    def S(call, *deps):
+        need("s", deps)
+        return did(call(g.scalar), "ss", 1)
+
+    def E(call, *deps):
+        need("t", deps)
+        return did(call(g.tensor), "ts", 1)
+
+    def I(call, *deps):
+        need("g", deps)
+        return did(call(g), "gs", 1)
+
+    def load(q, sem, out, in_, *deps):
+        need(q, deps)
+        return did(queue[q].dma_start(out, in_), sem, 16)
+
+    def mask(dst, quiet=False):
+        es = topo.engines(core, dst)
+        if quiet:
+            es = [e for e in es if e not in topo.engines(core, peers[2])] or es
+        m = 0
+        for e in es:
+            m |= 1 << e
+        return m, len(es)
+
+    def send(dst, out, in_, sem, *deps, quiet=False):
+        need("g", deps)
+        m, n = mask(dst, quiet)
+        rid, pid, _ = topo.addr(dst)
+        g.remote_dma(out, in_, T.sem[sem], T.sem["sent"], pid, rid, m)
+        total["sent"] = total.get("sent", 0) + n
+        total[sem] = total.get(sem, 0) + n
+        return (sem, total[sem])
+
+    def send_codes(dst, to, frm, a, b, sem, *deps):
+        return send(dst, T["c" + to][:, a:b].bitcast(dt.uint8), T["c" + frm][:, a:b].bitcast(dt.uint8), sem, *deps)
+
+    def send_scales(dst, to, frm, a, b, sem, *deps):
+        return send(dst, T["s" + to][:, a:b], T["s" + frm][:, a:b], sem, *deps)
+
+    def pick_c(to, a, b, frm, n, off, k, *deps):
+        return V(lambda q: q.tensor_copy(T["c" + to][:, a:b].bitcast(dt.uint32),
+                                         T["c" + frm][:, 0:n].bitcast(dt.uint32).indirect(T[off][:, 0:k])), *deps)
+
+    def pick_s(to, a, b, frm, n, off, k, *deps):
+        return S(lambda q: q.activation(T["s" + to][:, a:b], T["s" + frm][:, 0:n].indirect(T[off][:, 0:k]), F.Copy), *deps)
+
+    def pick_n(out, frm, n, off, k, *deps):
+        return S(lambda q: q.activation(out, T[frm][:, 0:n].indirect(T[off][:, 0:k]), F.Copy), *deps)
+
+    def quant(to, a, b, in_, *deps):
+        return V(lambda q: q.quantize_mx(T["c" + to][:, a:b], T["s" + to][:, a:b], in_), *deps)
+
+    dx = load("y", "dx", T.xt[:], T.x[:])
+    du = load("s", "du", T.ut[:], T.u[:, 0:4 * L])
+    dw = {0: [load("y", "dw0%d" % i, T.wt0[:, 512 * i:512 * i + 512], T.w[:, 512 * i:512 * i + 512]) for i in range(4)]}
+
+    zb = V(lambda q: q.memset(T.zb[:], 0.0))
+    c1 = V(lambda q: q.memset(T.cw[:, 0:NP], 1.0))
+    c2 = V(lambda q: q.memset(T.cw[:, NP:WIN], 0.0))
+    flag = {"allow_small_or_imprecise_dtypes": True}
+    iq = I(lambda q: q.iota(T.iq[:], [[0, 8]], 0, 1))
+    ic = I(lambda q: q.iota(T.ic[:], [[16, 8]], 0, 0, **flag))
+    ia = I(lambda q: q.iota(T.ia[:], [[1, 128]], 128, -1))
+    r0 = I(lambda q: q.iota(T.r0[:], [[0, 8], [1, 16]], 0, 0, **flag))
+    im = I(lambda q: q.iota(T.im0[:, 0:NP], [[1, NP]], rank * NP, 0, **flag))
+    iw = I(lambda q: q.iota(T.iw0[:, 0:NP], [[1, NP]], (rank ^ 1) * NP, 0, **flag))
+    p8, jb, jc = T.pj[:, 0:8], T.pj[:, 8:16], T.pj[:, 16:24]
+    ir = V(lambda q: q.tensor_scalar(T["ir"][:], T.iq[:], 15, None, A.bitwise_and), iq)
+    kp8 = V(lambda q: q.tensor_tensor(p8, T["ir"][:], T.ic[:], A.add), ir, ic)
+    kjb = V(lambda q: q.tensor_scalar(jb, p8, NP - 0.5, None, A.add), kp8)
+    kjc = V(lambda q: q.tensor_scalar(jc, p8, NP - 1.0, None, A.add), kp8)
+    ib = V(lambda q: q.tensor_scalar(T.ib[:], T.ia[:], 15, None, A.bitwise_and), ia)
+    th = V(lambda q: q.tensor_scalar(T.th[:], T.ib[:], 0.0, -1e29, A.not_equal, A.mult), ib)
+    rm = V(lambda q: q.tensor_scalar(T.rm[:], T.r0[:], 0.0, None, A.is_gt), r0)
+
+    def gauge(b):
+        return [S(lambda q: q.activation(T["gt%d" % b][:, t:512:4], T.zb[:], F.Identity, bias=T.ut[:, 4 * b + t:4 * b + t + 1]), zb, du)
+                for t in range(4)][-1]
+
+    gg = {0: gauge(0)}
+    Ac = As = quant("A0", 0, NP, T.xt[:], dx)
+    qg = {0: quant("G0", 0, NP, T.gt0[:], gg[0])}
+    Mc = Ms = quant("M0", 0, NP, T.xt[:], dx)
+
+    send_codes(peers[0], "P0", "A0", 0, NP, "ap0", Ac)
+    P = send_scales(peers[0], "P0", "A0", 0, NP, "ap0", As)
+    g.sem_inc(T.sem["gi"], 1)
+    total["gi"] = 1
+    dw[1] = [load("y", "dw1%d" % i, T.wt1[:, 1024 * i:1024 * i + 1024], T.w[:, 2048 + 1024 * i:3072 + 1024 * i], ("gi", 1)) for i in range(2)]
+
+    ids, idp = im, iw
+    casts, wants, qw, az, ccs, scs, ml = [None] * 4, (None, None), {}, [], [], [], None
+
+    def expert(b, *parts):
+        return [quant("W%d" % b, 128 * i, 128 * i + 128 * w, T["wt%d" % b][:, 512 * i:512 * i + 512 * w], d)
+                for i, w, d in parts][-1]
+
+    for b in range(L):
+        n = "%d" % b
+        sm, su, cc = T["sm" + n], T["su" + n], T["cc" + n]
+        sc = E(lambda q: q.matmul_mx(T.ps[:, 0:NP], T["cG" + n][:, 0:NP], T["sG" + n][:, 0:NP], T["cA" + n][:, 0:NP], T["sA" + n][:, 0:NP],
+                                     True, True), qg[b], Ac, As, *wants)
+        wa = V(lambda q: q.tensor_scalar(T["wa" + n][:], T.ps[:, 0:NP], 0.0, None, A.is_lt), sc)
+        ct = V(lambda q: q.tensor_tensor_scan(cc[:], T["wa" + n][:], T["wa" + n][:], NP - 1.0, A.add, A.max), wa)
+        ccs.append(ct)
+        if b == 1:
+            ids = pick_n(T.im1[:, 0:NP], "im0", WIN, "ml0", 8, idn, ids, ml)
+        sums = [S(lambda q: q.activation(T["jk" + n][:, NP * c:NP * c + NP], cc[:], F.Sign, bias=jb[:, c:c + 1] if False else T.pj[:, 8 + c:9 + c],
+                                         scale=-1.0, accum_out=su[:, c:c + 1]), ct, kjb) for c in range(3)]
+        t = V(lambda q: q.tensor_scalar(sm[:, 0:3], T.pj[:, 16:19], cc[:, NP - 1:NP], None, A.is_ge), ct, kjc)
+        t = V(lambda q: q.tensor_tensor(sm[:, 4:7], sm[:, 0:3], T.pj[:, 0:3], A.mult), t)
+        t = V(lambda q: q.tensor_scalar(sm[:, 8:11], sm[:, 4:7], 64.0, None, A.add), t)
+        if b == 2:
+            base = float(NP * ((rank ^ 2) & ~1))
+            e = V(lambda q: q.tensor_copy(T.ui[:, 0:2], T.pl[:, 0:2]), ai1)
+            e1 = V(lambda q: q.tensor_scalar(T.uj[:, 0:2], T.ui[:, 0:2], 8, None, A.logical_shift_right), e)
+            e2 = V(lambda q: q.tensor_scalar(T.uj[:, 4:6], T.ui[:, 0:2], 255, None, A.bitwise_and), e)
+            e1 = V(lambda q: q.tensor_scalar(T.un[:, 0:2], T.uj[:, 0:2], base, None, A.add), e1)
+            e2 = V(lambda q: q.tensor_scalar(T.un[:, 2:4], T.uj[:, 4:6], base, None, A.add), e2)
+        z = [V(lambda q: q.tensor_scalar(T["zz" + n][:, c:c + 1], su[:, c:c + 1], 0.5, sm[:, 8 + c:9 + c], A.mult, A.add), t, sums[c])
+             for c in range(3)][-1]
+        az.append(send(peers[b], T["lz" + n][:, 0:3], T["zz" + n][:, 0:3], "az" + n, z, quiet=(b == 1)))
+        lo = V(lambda q: q.tensor_scalar(T["lo" + n][:, 0:3], T["zz" + n][:, 0:3], float(NP - 1), None, A.min), z)
+        if b == 2:
+            ex = [S(lambda q: q.activation(T.ex[:, 32 * m:32 * m + 32], T.zb[:, 0:32], F.Identity, bias=T.un[:, m:m + 1]), e1, e2)
+                  for m in range(4)][-1]
+            idp = V(lambda q: q.transpose(T.iw1[:, 0:NP], T.ex[:, 0:NP]), ex)
+            idn = pick_n(T.im1[:, NP:WIN], "iw1", WIN, "lz1", 3, idp, idw, az[1])
+            ids = pick_n(T.im2[:, 0:NP], "im1", WIN, "ml1", 8, idn, ids, ml)
+        xc = pick_c("X" + n, NP, WIN, "A" + n, NP, "lo" + n, 3, lo, Ac)
+        xs = pick_s("X" + n, NP, WIN, "A" + n, NP, "lo" + n, 3, lo, As)
+        idw = pick_n(T["iw" + n][:, NP:WIN], "im" + n, NP, "lo" + n, 3, lo, ids)
+        if b == 0:
+            gg[1], gg[2] = gauge(1), gauge(2)
+        if b == 1:
+            base = float(NP * (rank & ~1))
+            e = V(lambda q: q.transpose(T.it[:, 0:NP], T.im1[:, 0:NP]), ids)
+            e1 = V(lambda q: q.tensor_scalar(T.pa[:, 0:2], T.it[:, 0:64:32], 256.0, -257.0 * base, A.mult, A.add), e)
+            e1 = V(lambda q: q.tensor_tensor(T.pa[:, 4:6], T.pa[:, 0:2], T.it[:, 64:128:32], A.add), e1)
+            e1 = V(lambda q: q.tensor_copy(T.px[:, 0:2], T.pa[:, 4:6]), e1)
+            ai1 = send(peers[1], T.pl[:, 0:2], T.px[:, 0:2], "ai1", e1, quiet=True)
+        if b == 2:
+            e = V(lambda q: q.tensor_copy(T.ui[:, 4:8], T.mxl[:]), aml)
+            e1 = V(lambda q: q.tensor_scalar(T.uj[:, 8:12], T.ui[:, 4:8], 8, None, A.logical_shift_right), e)
+            e2 = V(lambda q: q.tensor_scalar(T.uj[:, 12:16], T.ui[:, 4:8], 255, None, A.bitwise_and), e)
+            e1 = V(lambda q: q.tensor_copy(T.pm[:, 0:4], T.uj[:, 8:12]), e1)
+            pm = V(lambda q: q.tensor_copy(T.pm[:, 4:8], T.uj[:, 12:16]), e2)
+            qw[2] = expert(2, (0, 2, dw[2][0]), (2, 2, dw[2][1]))
+            e = V(lambda q: q.transpose(T.it[:, NP:2 * NP], T.im2[:, 0:NP]), ids)
+            e = V(lambda q: q.tensor_copy(T.qx[:], T.it[:, NP:2 * NP:32]), e)
+            ai2 = send(peers[2], T.ql[:], T.qx[:], "ai2", e)
+            Pd = (pick_c("P2", 0, NP, "R", WIN, "pm", 8, pm, ar0, ar1), pick_s("P2", 0, NP, "R", WIN, "pm", 8, pm, ar0, ar1))
+        else:
+            Pd = (P,)
+        wd = V(lambda q: q.tensor_tensor(T["wd" + n][:], T.ps[:, 0:NP], T.th[:], A.is_lt), sc, th)
+        yd = V(lambda q: q.tensor_tensor(T["yd" + n][:], T["wd" + n][:], cc[:], A.mult), wd, ct)
+        dd = V(lambda q: q.tensor_tensor_scan(T["dd" + n][:], T.rm[:], T["yd" + n][:], 0.0, A.mult, A.add), yd, rm)
+        d8 = T["dd" + n][:, 15:128:16]
+        t = V(lambda q: q.tensor_scalar(sm[:, 16:24], d8, float(WIN - 1), None, A.is_le), dd)
+        t = V(lambda q: q.tensor_tensor(sm[:, 24:32], sm[:, 16:24], d8, A.mult), t)
+        t = V(lambda q: q.tensor_tensor(sm[:, 32:40], sm[:, 24:32], T.pj[:, 0:8], A.max), t, kp8)
+        ml = V(lambda q: q.tensor_copy(T["ml" + n][:], sm[:, 32:40]), t)
+        wants = (wa, wd)
+        if b == 0:
+            qg[1] = quant("G1", 0, NP, T.gt1[:], gg[1])
+            qg[2] = quant("G2", 0, NP, T.gt2[:], gg[2])
+            qw[0] = expert(0, *[(i, 1, dw[0][i]) for i in range(4)])
+        if b == 1:
+            e = V(lambda q: q.tensor_scalar(sm[:, 40:44], sm[:, 32:36], 256.0, None, A.mult), t)
+            e = V(lambda q: q.tensor_tensor(sm[:, 44:48], sm[:, 40:44], sm[:, 36:40], A.add), e)
+            e = V(lambda q: q.tensor_copy(T.mx1[:], sm[:, 44:48]), e)
+            aml = send(peers[2], T.mxl[:], T.mx1[:], "aml", e)
+            qw[1] = expert(1, (0, 2, dw[1][0]), (2, 2, dw[1][1]))
+        if b == 2:
+            qv = quant("V", 0, NP, T.vt[:], dv)
+        h = T["ht" + n]
+        mm = [E(lambda q: q.matmul_mx(T.pe[:, 512 * i:512 * i + NP], T["cW" + n][:, 128 * i:128 * i + 128], T["sW" + n][:, 128 * i:128 * i + 128],
+                                      T["cP" + n][:, 0:NP], T["sP" + n][:, 0:NP], True, True), qw[b], casts[i], *Pd) for i in range(4)]
+        for i in range(4):
+            if i == 2:
+                casts[i] = V(lambda q: q.tensor_scalar(h[:, i:512:4], T.pe[:, 512 * i:512 * i + NP], 0.0625, None, A.mult), mm[i])
+            else:
+                casts[i] = S(lambda q: q.activation(h[:, i:512:4], T.pe[:, 512 * i:512 * i + NP], F.Copy, scale=0.0625), mm[i])
+        qn = quant("X" + n, 0, NP, h[:], *casts)
+        if b == 0:
+            idn = pick_n(T.im0[:, NP:WIN], "iw0", WIN, "lz0", 3, idp, idw, az[0])
+        nc = pick_c("M" + n, NP, WIN, "X" + n, WIN, "lz" + n, 3, qn, xc, az[b])
+        ns = pick_s("M" + n, NP, WIN, "X" + n, WIN, "lz" + n, 3, qn, xs, az[b])
+        if b == 1:
+            send_codes(peers[2], "R", "M1", NP, WIN, "ar1", nc)
+            ar1 = send_scales(peers[2], "R", "M1", NP, WIN, "ar1", ns)
+        o = "%d" % (b + 1)
+        Ac = pick_c("A" + o, 0, NP, "M" + n, WIN, "ml" + n, 8, nc, ml, Mc)
+        As = pick_s("A" + o, 0, NP, "M" + n, WIN, "ml" + n, 8, ns, ml, Ms)
+        if b < 2:
+            Mc, Ms = pick_c("M" + o, 0, NP, "M" + n, WIN, "ml" + n, 8), pick_s("M" + o, 0, NP, "M" + n, WIN, "ml" + n, 8)
+        if b == 0:
+            send_codes(peers[1], "P1", "A1", 0, NP, "ap1", Ac)
+            P = send_scales(peers[1], "P1", "A1", 0, NP, "ap1", As)
+            send_codes(peers[2], "R", "A1", 0, NP, "ar0", Ac)
+            ar0 = send_scales(peers[2], "R", "A1", 0, NP, "ar0", As)
+            g.sem_inc(T.sem["gi"], 1)
+            total["gi"] = 2
+            dw[2] = [load("y", "dw2%d" % i, T.wt2[:, 1024 * i:1024 * i + 1024], T.w[:, 4096 + 1024 * i:5120 + 1024 * i], ("gi", 2)) for i in range(2)]
+            dv = load("y", "dv", T.vt[:], T.v[:])
+
+    ym = E(lambda q: q.matmul_mx(T.py[:, 0:NP], T.cV[:, 0:NP], T.sV[:, 0:NP], T.cA3[:, 0:NP], T.sA3[:, 0:NP], True, True), qv, Ac, As)
+    load("y", "out", T.oc[:, 0:4 * NP], T.cA3[:, 0:NP].bitcast(dt.uint8), Ac)
+    for k in range(4):
+        load("y", "out", T.osc[4 * k:4 * k + 4, 0:NP], T.sA3[32 * k:32 * k + 4, 0:NP], As)
+    yt = V(lambda q: q.tensor_copy(T.yt[:], T.py[:, 0:NP]), ym)
+    load("y", "out", T.y[:], T.yt[:], yt)
+    e = V(lambda q: q.tensor_copy(T.un[:, 4:8], T.ql[:]), ai2)
+    ex = [S(lambda q: q.activation(T.ex[:, NP + 32 * m:NP + 32 * m + 32], T.zb[:, 0:32], F.Identity, bias=T.un[:, 4 + m:5 + m]), e)
+          for m in range(4)][-1]
+    idp = V(lambda q: q.transpose(T.iw2[:, 0:NP], T.ex[:, NP:2 * NP]), ex)
+    kp = [S(lambda q: q.activation(T.kj[:, CAPP * b:CAPP * b + CAPP], T.cw[:, 0:WIN].indirect(T["lz%d" % b][:, 0:3]), F.Copy,
+                                   accum_out=T.kk[:, b:b + 1]), c1, c2, az[b]) for b in range(L)]
+    idn = pick_n(T.im2[:, NP:WIN], "iw2", WIN, "lz2", 3, idp, idw, az[2])
+    idf = pick_n(T.idf[:], "im2", WIN, "ml2", 8, idn, ids, ml)
+    kk = [V(lambda q: q.tensor_scalar(T.kk[:, 4 + b:5 + b], T.kk[:, b:b + 1], NP - 1.0, T["cc%d" % b][:, NP - 1:NP], A.add, A.min), kp[b], ccs[b])
+          for b in range(L)][-1]
+    kk = V(lambda q: q.tensor_scalar(T.kk[:, 8:8 + L], T.kk[:, 4:4 + L], 1.0 - NP, None, A.add), kk)
+    load("y", "out", T.ks[:], T.kk[0:1, 8:8 + L], kk)
+    load("y", "out", T.ids[:], T.idf[0:1, :], idf)
+
+    for s in sorted(total):
+        need("g", [(s, total[s])])

@@ -1,10 +1,10 @@
-from concourse.bass import DstId, RemoteDMATransfer
-from concourse.mybir import dt, AluOpType, AxisListType, ActivationFunctionType
+from concourse.mybir import dt, AluOpType, ActivationFunctionType
 
 L, CAPP, NP = 3, 48, 128
 WIN = NP + CAPP
 A = AluOpType
 F = ActivationFunctionType
+LOADS = {"x": [(0, 0, 2), (0, 2, 2), (1, 0, 4), (L, 0, 0)], "p0": [(2, 0, 4)]}
 
 SCRATCH = {}
 
@@ -73,7 +73,6 @@ _sb("mxl", 4, "uint16")
 _sb("pm", 8, "uint16")
 _sb("ui", 16, "int32")
 _sb("uj", 16, "int32")
-_sb("un", 8)
 _sb("ex", 256)
 _sb("idf", 128)
 _sb("kk", 12)
@@ -82,8 +81,8 @@ SCRATCH["pe"] = ("psum", [128, 2048], "float32")
 SCRATCH["ps"] = ("psum", [128, 512], "float32")
 SCRATCH["py"] = ("psum", [128, 512], "float32")
 
-SEMAPHORES = (["vs", "ss", "ts", "gs", "gi", "sent", "dx", "du", "dv", "out"]
-              + ["dw0%d" % i for i in range(4)] + ["dw%d%d" % (b, i) for b in (1, 2) for i in range(2)]
+SEMAPHORES = (["vs", "ss", "ts", "gs", "gi", "sent", "dx", "du", "dv", "out", "dm0", "dm1"]
+              + ["dw%d%d" % (b, i) for b in range(L) for i in range(4)]
               + ["ap0", "ap1", "ar0", "ar1", "az0", "az1", "az2", "ai1", "ai2", "aml"])
 
 
@@ -168,9 +167,25 @@ def rank_program(g, core, T, topo):
 
     dx = load("y", "dx", T.xt[:], T.x[:])
     du = load("s", "du", T.ut[:], T.u[:, 0:4 * L])
-    dw = {0: [load("y", "dw0%d" % i, T.wt0[:, 512 * i:512 * i + 512], T.w[:, 512 * i:512 * i + 512]) for i in range(4)]}
+    dw = {b: {} for b in range(L + 1)}
+
+    def issued():
+        g.sem_inc(T.sem["gi"], 1)
+        total["gi"] = total.get("gi", 0) + 1
+        return ("gi", total["gi"])
+
+    def point(name, *deps):
+        for b, i, w in LOADS[name]:
+            if b == L:
+                dw[b][i, w] = load("y", "dv", T.vt[:], T.v[:], *deps)
+            else:
+                dw[b][i, w] = load("y", "dw%d%d" % (b, i), T["wt%d" % b][:, 512 * i:512 * i + 512 * w],
+                                   T.w[:, 2048 * b + 512 * i:2048 * b + 512 * i + 512 * w], *deps)
+
+    point("x")
 
     zb = V(lambda q: q.memset(T.zb[:], 0.0))
+    zx = V(lambda q: q.memset(T.ex[:], 0.0))
     c1 = V(lambda q: q.memset(T.cw[:, 0:NP], 1.0))
     c2 = V(lambda q: q.memset(T.cw[:, NP:WIN], 0.0))
     flag = {"allow_small_or_imprecise_dtypes": True}
@@ -200,144 +215,199 @@ def rank_program(g, core, T, topo):
 
     send_codes(peers[0], "P0", "A0", 0, NP, "ap0", Ac)
     P = send_scales(peers[0], "P0", "A0", 0, NP, "ap0", As)
-    g.sem_inc(T.sem["gi"], 1)
-    total["gi"] = 1
-    dw[1] = [load("y", "dw1%d" % i, T.wt1[:, 1024 * i:1024 * i + 1024], T.w[:, 2048 + 1024 * i:3072 + 1024 * i], ("gi", 1)) for i in range(2)]
 
     ids, idp = im, iw
-    casts, wants, qw, az, ccs, scs, ml = [None] * 4, (None, None), {}, [], [], [], None
+    k = {"wa": None, "wd": None, "ml": None}
+    casts, az, ccs, kp = [None] * 4, [], [], []
 
-    def expert(b, *parts):
-        return [quant("W%d" % b, 128 * i, 128 * i + 128 * w, T["wt%d" % b][:, 512 * i:512 * i + 512 * w], d)
-                for i, w, d in parts][-1]
+    def turns(*chains):
+        chains = list(chains)
+        while chains:
+            chains = [c for c in chains if next(c, 0)]
+
+    def count(b):
+        kp.append(S(lambda q: q.activation(T.kj[:, CAPP * b:CAPP * b + CAPP], T.cw[:, 0:WIN].indirect(T["lz%d" % b][:, 0:3]), F.Copy,
+                                           accum_out=T.kk[:, b:b + 1]), c1, c2, az[b]))
+
+    def expert(b):
+        for i in range(4):
+            d = [t for (j, w), t in dw[b].items() if j <= i < j + w]
+            k["qw%d" % b] = quant("W%d" % b, 128 * i, 128 * i + 128, T["wt%d" % b][:, 512 * i:512 * i + 512], *d)
+
+    def own_list(b):
+        n = "%d" % b
+        sm, su, cc = T["sm" + n], T["su" + n], T["cc" + n]
+        k["wa"] = V(lambda q: q.tensor_scalar(T["wa" + n][:], T.ps[:, 0:NP], 0.0, None, A.is_lt), k["sc"])
+        yield 1
+        k["ct"] = V(lambda q: q.tensor_tensor_scan(cc[:], T["wa" + n][:], T["wa" + n][:], NP - 1.0, A.add, A.max), k["wa"])
+        ccs.append(k["ct"])
+        sums = [S(lambda q: q.activation(T["jk" + n][:, NP * c:NP * c + NP], cc[:], F.Sign, bias=T.pj[:, 8 + c:9 + c], scale=-1.0,
+                                         accum_out=su[:, c:c + 1]), k["ct"], kjb) for c in range(3)]
+        yield 1
+        for c in range(3):
+            t = V(lambda q: q.tensor_scalar(sm[:, c:c + 1], cc[:, NP - 1:NP], T.pj[:, 16 + c:17 + c], T.pj[:, c:c + 1], A.is_le, A.mult),
+                  k["ct"], kjc)
+        yield 1
+        t = V(lambda q: q.tensor_scalar(sm[:, 8:11], sm[:, 0:3], 64.0, None, A.add), t)
+        yield 1
+        for c in range(3):
+            z = V(lambda q: q.tensor_scalar(T["zz" + n][:, c:c + 1], su[:, c:c + 1], 0.5, sm[:, 8 + c:9 + c], A.mult, A.add), t, sums[c])
+        az.append(send(peers[b], T["lz" + n][:, 0:3], T["zz" + n][:, 0:3], "az" + n, z, quiet=(b == 1)))
+        yield 1
+        lo = k["lo"] = V(lambda q: q.tensor_scalar(T["lo" + n][:, 0:3], T["zz" + n][:, 0:3], float(NP - 1), None, A.min), z)
+        yield 1
+        k["xc"] = pick_c("X" + n, NP, WIN, "A" + n, NP, "lo" + n, 3, lo, Ac)
+        k["xs"] = pick_s("X" + n, NP, WIN, "A" + n, NP, "lo" + n, 3, lo, As)
+        yield 1
+
+    def merging_list(b):
+        n = "%d" % b
+        sm, cc = T["sm" + n], T["cc" + n]
+        k["wd"] = V(lambda q: q.tensor_tensor(T["wd" + n][:], T.ps[:, 0:NP], T.th[:], A.is_lt), k["sc"], th)
+        yield 1
+        yield 1
+        t = V(lambda q: q.tensor_tensor(T["yd" + n][:], T["wd" + n][:], cc[:], A.mult), k["wd"], k["ct"])
+        yield 1
+        t = V(lambda q: q.tensor_tensor_scan(T["dd" + n][:], T.rm[:], T["yd" + n][:], 0.0, A.mult, A.add), t, rm)
+        yield 1
+        d8 = T["dd" + n][:, 15:128:16]
+        t = V(lambda q: q.tensor_scalar(sm[:, 16:24], d8, float(WIN - 1), None, A.is_le), t)
+        yield 1
+        t = V(lambda q: q.tensor_tensor(sm[:, 24:32], sm[:, 16:24], d8, A.mult), t)
+        yield 1
+        t = V(lambda q: q.tensor_tensor(sm[:, 32:40], sm[:, 24:32], T.pj[:, 0:8], A.max), t, kp8)
+        yield 1
+        k["ml"] = V(lambda q: q.tensor_copy(T["ml" + n][:], sm[:, 32:40]), t)
+        if b == 1:
+            t = V(lambda q: q.tensor_scalar(sm[:, 40:44], sm[:, 32:36], 256.0, None, A.mult), t)
+            yield 1
+            t = V(lambda q: q.tensor_tensor(sm[:, 44:48], sm[:, 40:44], sm[:, 36:40], A.add), t)
+            yield 1
+            t = V(lambda q: q.tensor_copy(T.mx1[:], sm[:, 44:48]), t)
+            k["aml"] = send(peers[2], T.mxl[:], T.mx1[:], "aml", t)
+        yield 1
+
+    def send_numbers():
+        base = float(NP * (rank & ~1))
+        for _ in range(5):
+            yield 1
+        t = V(lambda q: q.transpose(T.it[:, 0:NP], T.im1[:, 0:NP]), ids)
+        yield 1
+        t = V(lambda q: q.tensor_scalar(T.pa[:, 0:2], T.it[:, 0:64:32], 256.0, -257.0 * base, A.mult, A.add), t)
+        yield 1
+        t = V(lambda q: q.tensor_tensor(T.pa[:, 4:6], T.pa[:, 0:2], T.it[:, 64:128:32], A.add), t)
+        yield 1
+        t = V(lambda q: q.tensor_copy(T.px[:, 0:2], T.pa[:, 4:6]), t)
+        k["ai1"] = send(peers[1], T.pl[:, 0:2], T.px[:, 0:2], "ai1", t, quiet=True)
+        yield 1
+
+    def take_numbers():
+        base = float(NP * ((rank ^ 2) & ~1))
+        yield 1
+        yield 1
+        e = V(lambda q: q.tensor_copy(T.ui[:, 0:2], T.pl[:, 0:2]), k["ai1"])
+        yield 1
+        e1 = V(lambda q: q.tensor_scalar(T.uj[:, 0:2], T.ui[:, 0:2], 8, None, A.logical_shift_right), e)
+        e2 = V(lambda q: q.tensor_scalar(T.uj[:, 4:6], T.ui[:, 0:2], 255, None, A.bitwise_and), e)
+        yield 1
+        e1 = V(lambda q: q.tensor_scalar(T.ex[:, 0:64:32], T.uj[:, 0:2], base, None, A.add), e1, zx)
+        e2 = V(lambda q: q.tensor_scalar(T.ex[:, 64:128:32], T.uj[:, 4:6], base, None, A.add), e2)
+        yield 1
+        k["idp"] = V(lambda q: q.transpose(T.iw1[:, 0:NP], T.ex[:, 0:NP]), e1, e2)
+        yield 1
+
+    def take_list():
+        for _ in range(3):
+            yield 1
+        e = V(lambda q: q.tensor_copy(T.ui[:, 4:8], T.mxl[:]), k["aml"])
+        yield 1
+        e1 = V(lambda q: q.tensor_scalar(T.uj[:, 8:12], T.ui[:, 4:8], 8, None, A.logical_shift_right), e)
+        e2 = V(lambda q: q.tensor_scalar(T.uj[:, 12:16], T.ui[:, 4:8], 255, None, A.bitwise_and), e)
+        yield 1
+        e1 = V(lambda q: q.tensor_copy(T.pm[:, 0:4], T.uj[:, 8:12]), e1)
+        k["pm"] = V(lambda q: q.tensor_copy(T.pm[:, 4:8], T.uj[:, 12:16]), e2)
+        yield 1
 
     for b in range(L):
         n = "%d" % b
-        sm, su, cc = T["sm" + n], T["su" + n], T["cc" + n]
-        sc = E(lambda q: q.matmul_mx(T.ps[:, 0:NP], T["cG" + n][:, 0:NP], T["sG" + n][:, 0:NP], T["cA" + n][:, 0:NP], T["sA" + n][:, 0:NP],
-                                     True, True), qg[b], Ac, As, *wants)
-        wa = V(lambda q: q.tensor_scalar(T["wa" + n][:], T.ps[:, 0:NP], 0.0, None, A.is_lt), sc)
-        ct = V(lambda q: q.tensor_tensor_scan(cc[:], T["wa" + n][:], T["wa" + n][:], NP - 1.0, A.add, A.max), wa)
-        ccs.append(ct)
         if b == 1:
-            ids = pick_n(T.im1[:, 0:NP], "im0", WIN, "ml0", 8, idn, ids, ml)
-        sums = [S(lambda q: q.activation(T["jk" + n][:, NP * c:NP * c + NP], cc[:], F.Sign, bias=jb[:, c:c + 1] if False else T.pj[:, 8 + c:9 + c],
-                                         scale=-1.0, accum_out=su[:, c:c + 1]), ct, kjb) for c in range(3)]
-        t = V(lambda q: q.tensor_scalar(sm[:, 0:3], T.pj[:, 16:19], cc[:, NP - 1:NP], None, A.is_ge), ct, kjc)
-        t = V(lambda q: q.tensor_tensor(sm[:, 4:7], sm[:, 0:3], T.pj[:, 0:3], A.mult), t)
-        t = V(lambda q: q.tensor_scalar(sm[:, 8:11], sm[:, 4:7], 64.0, None, A.add), t)
-        if b == 2:
-            base = float(NP * ((rank ^ 2) & ~1))
-            e = V(lambda q: q.tensor_copy(T.ui[:, 0:2], T.pl[:, 0:2]), ai1)
-            e1 = V(lambda q: q.tensor_scalar(T.uj[:, 0:2], T.ui[:, 0:2], 8, None, A.logical_shift_right), e)
-            e2 = V(lambda q: q.tensor_scalar(T.uj[:, 4:6], T.ui[:, 0:2], 255, None, A.bitwise_and), e)
-            e1 = V(lambda q: q.tensor_scalar(T.un[:, 0:2], T.uj[:, 0:2], base, None, A.add), e1)
-            e2 = V(lambda q: q.tensor_scalar(T.un[:, 2:4], T.uj[:, 4:6], base, None, A.add), e2)
-        z = [V(lambda q: q.tensor_scalar(T["zz" + n][:, c:c + 1], su[:, c:c + 1], 0.5, sm[:, 8 + c:9 + c], A.mult, A.add), t, sums[c])
-             for c in range(3)][-1]
-        az.append(send(peers[b], T["lz" + n][:, 0:3], T["zz" + n][:, 0:3], "az" + n, z, quiet=(b == 1)))
-        lo = V(lambda q: q.tensor_scalar(T["lo" + n][:, 0:3], T["zz" + n][:, 0:3], float(NP - 1), None, A.min), z)
-        if b == 2:
-            ex = [S(lambda q: q.activation(T.ex[:, 32 * m:32 * m + 32], T.zb[:, 0:32], F.Identity, bias=T.un[:, m:m + 1]), e1, e2)
-                  for m in range(4)][-1]
-            idp = V(lambda q: q.transpose(T.iw1[:, 0:NP], T.ex[:, 0:NP]), ex)
-            idn = pick_n(T.im1[:, NP:WIN], "iw1", WIN, "lz1", 3, idp, idw, az[1])
-            ids = pick_n(T.im2[:, 0:NP], "im1", WIN, "ml1", 8, idn, ids, ml)
-        xc = pick_c("X" + n, NP, WIN, "A" + n, NP, "lo" + n, 3, lo, Ac)
-        xs = pick_s("X" + n, NP, WIN, "A" + n, NP, "lo" + n, 3, lo, As)
-        idw = pick_n(T["iw" + n][:, NP:WIN], "im" + n, NP, "lo" + n, 3, lo, ids)
+            ids = pick_n(T.im1[:, 0:NP], "im0", WIN, "ml0", 8, idn, ids, k["ml"])
+        k["sc"] = E(lambda q: q.matmul_mx(T.ps[:, 0:NP], T["cG" + n][:, 0:NP], T["sG" + n][:, 0:NP], T["cA" + n][:, 0:NP],
+                                          T["sA" + n][:, 0:NP], True, True), qg[b], Ac, As, k["wa"], k["wd"])
+        Pd, old = (P,), k["ml"]
         if b == 0:
-            gg[1], gg[2] = gauge(1), gauge(2)
+            turns(own_list(0), merging_list(0))
+            point("p0", P)
         if b == 1:
-            base = float(NP * (rank & ~1))
-            e = V(lambda q: q.transpose(T.it[:, 0:NP], T.im1[:, 0:NP]), ids)
-            e1 = V(lambda q: q.tensor_scalar(T.pa[:, 0:2], T.it[:, 0:64:32], 256.0, -257.0 * base, A.mult, A.add), e)
-            e1 = V(lambda q: q.tensor_tensor(T.pa[:, 4:6], T.pa[:, 0:2], T.it[:, 64:128:32], A.add), e1)
-            e1 = V(lambda q: q.tensor_copy(T.px[:, 0:2], T.pa[:, 4:6]), e1)
-            ai1 = send(peers[1], T.pl[:, 0:2], T.px[:, 0:2], "ai1", e1, quiet=True)
+            turns(own_list(1), merging_list(1), send_numbers())
         if b == 2:
-            e = V(lambda q: q.tensor_copy(T.ui[:, 4:8], T.mxl[:]), aml)
-            e1 = V(lambda q: q.tensor_scalar(T.uj[:, 8:12], T.ui[:, 4:8], 8, None, A.logical_shift_right), e)
-            e2 = V(lambda q: q.tensor_scalar(T.uj[:, 12:16], T.ui[:, 4:8], 255, None, A.bitwise_and), e)
-            e1 = V(lambda q: q.tensor_copy(T.pm[:, 0:4], T.uj[:, 8:12]), e1)
-            pm = V(lambda q: q.tensor_copy(T.pm[:, 4:8], T.uj[:, 12:16]), e2)
-            qw[2] = expert(2, (0, 2, dw[2][0]), (2, 2, dw[2][1]))
+            expert(2)
+            turns(own_list(2), take_numbers(), take_list(), merging_list(2))
+        if b < 2:
+            idw = pick_n(T["iw" + n][:, NP:WIN], "im" + n, NP, "lo" + n, 3, k["lo"], ids)
+        if b == 0:
+            for j in (1, 2):
+                gg[j] = gauge(j)
+            expert(0)
+            for j in (1, 2):
+                qg[j] = quant("G%d" % j, 0, NP, T["gt%d" % j][:], gg[j])
+        if b == 2:
+            Pd = (pick_c("P2", 0, NP, "R", WIN, "pm", 8, k["pm"], ar0, ar1), pick_s("P2", 0, NP, "R", WIN, "pm", 8, k["pm"], ar0, ar1))
+            idn = pick_n(T.im1[:, NP:WIN], "iw1", WIN, "lz1", 3, k["idp"], idw, az[1])
+            ids = pick_n(T.im2[:, 0:NP], "im1", WIN, "ml1", 8, idn, ids, old)
             e = V(lambda q: q.transpose(T.it[:, NP:2 * NP], T.im2[:, 0:NP]), ids)
             e = V(lambda q: q.tensor_copy(T.qx[:], T.it[:, NP:2 * NP:32]), e)
             ai2 = send(peers[2], T.ql[:], T.qx[:], "ai2", e)
-            Pd = (pick_c("P2", 0, NP, "R", WIN, "pm", 8, pm, ar0, ar1), pick_s("P2", 0, NP, "R", WIN, "pm", 8, pm, ar0, ar1))
-        else:
-            Pd = (P,)
-        wd = V(lambda q: q.tensor_tensor(T["wd" + n][:], T.ps[:, 0:NP], T.th[:], A.is_lt), sc, th)
-        yd = V(lambda q: q.tensor_tensor(T["yd" + n][:], T["wd" + n][:], cc[:], A.mult), wd, ct)
-        dd = V(lambda q: q.tensor_tensor_scan(T["dd" + n][:], T.rm[:], T["yd" + n][:], 0.0, A.mult, A.add), yd, rm)
-        d8 = T["dd" + n][:, 15:128:16]
-        t = V(lambda q: q.tensor_scalar(sm[:, 16:24], d8, float(WIN - 1), None, A.is_le), dd)
-        t = V(lambda q: q.tensor_tensor(sm[:, 24:32], sm[:, 16:24], d8, A.mult), t)
-        t = V(lambda q: q.tensor_tensor(sm[:, 32:40], sm[:, 24:32], T.pj[:, 0:8], A.max), t, kp8)
-        ml = V(lambda q: q.tensor_copy(T["ml" + n][:], sm[:, 32:40]), t)
-        wants = (wa, wd)
-        if b == 0:
-            qg[1] = quant("G1", 0, NP, T.gt1[:], gg[1])
-            qg[2] = quant("G2", 0, NP, T.gt2[:], gg[2])
-            qw[0] = expert(0, *[(i, 1, dw[0][i]) for i in range(4)])
-        if b == 1:
-            e = V(lambda q: q.tensor_scalar(sm[:, 40:44], sm[:, 32:36], 256.0, None, A.mult), t)
-            e = V(lambda q: q.tensor_tensor(sm[:, 44:48], sm[:, 40:44], sm[:, 36:40], A.add), e)
-            e = V(lambda q: q.tensor_copy(T.mx1[:], sm[:, 44:48]), e)
-            aml = send(peers[2], T.mxl[:], T.mx1[:], "aml", e)
-            qw[1] = expert(1, (0, 2, dw[1][0]), (2, 2, dw[1][1]))
-        if b == 2:
-            qv = quant("V", 0, NP, T.vt[:], dv)
         h = T["ht" + n]
         mm = [E(lambda q: q.matmul_mx(T.pe[:, 512 * i:512 * i + NP], T["cW" + n][:, 128 * i:128 * i + 128], T["sW" + n][:, 128 * i:128 * i + 128],
-                                      T["cP" + n][:, 0:NP], T["sP" + n][:, 0:NP], True, True), qw[b], casts[i], *Pd) for i in range(4)]
-        for i in range(4):
-            if i == 2:
-                casts[i] = V(lambda q: q.tensor_scalar(h[:, i:512:4], T.pe[:, 512 * i:512 * i + NP], 0.0625, None, A.mult), mm[i])
-            else:
-                casts[i] = S(lambda q: q.activation(h[:, i:512:4], T.pe[:, 512 * i:512 * i + NP], F.Copy, scale=0.0625), mm[i])
+                                      T["cP" + n][:, 0:NP], T["sP" + n][:, 0:NP], True, True), k["qw" + n], casts[i], *Pd) for i in range(4)]
+        for i in range(3):
+            casts[i] = S(lambda q: q.activation(h[:, i:512:4], T.pe[:, 512 * i:512 * i + NP], F.Copy, scale=0.0625), mm[i])
+        if b == 0:
+            expert(1)
+        casts[3] = V(lambda q: q.tensor_scalar(h[:, 3:512:4], T.pe[:, 1536:1536 + NP], 0.0625, None, A.mult), mm[3])
         qn = quant("X" + n, 0, NP, h[:], *casts)
         if b == 0:
             idn = pick_n(T.im0[:, NP:WIN], "iw0", WIN, "lz0", 3, idp, idw, az[0])
-        nc = pick_c("M" + n, NP, WIN, "X" + n, WIN, "lz" + n, 3, qn, xc, az[b])
-        ns = pick_s("M" + n, NP, WIN, "X" + n, WIN, "lz" + n, 3, qn, xs, az[b])
+        if b == 1:
+            qv = quant("V", 0, NP, T.vt[:], *dw[L].values())
+        if b == 2:
+            idw = pick_n(T.iw2[:, NP:WIN], "im2", NP, "lo2", 3, k["lo"], ids)
+            for j in range(L):
+                count(j)
+        nc = pick_c("M" + n, NP, WIN, "X" + n, WIN, "lz" + n, 3, qn, k["xc"], az[b])
+        ns = pick_s("M" + n, NP, WIN, "X" + n, WIN, "lz" + n, 3, qn, k["xs"], az[b])
         if b == 1:
             send_codes(peers[2], "R", "M1", NP, WIN, "ar1", nc)
             ar1 = send_scales(peers[2], "R", "M1", NP, WIN, "ar1", ns)
         o = "%d" % (b + 1)
-        Ac = pick_c("A" + o, 0, NP, "M" + n, WIN, "ml" + n, 8, nc, ml, Mc)
-        As = pick_s("A" + o, 0, NP, "M" + n, WIN, "ml" + n, 8, ns, ml, Ms)
-        if b < 2:
-            Mc, Ms = pick_c("M" + o, 0, NP, "M" + n, WIN, "ml" + n, 8), pick_s("M" + o, 0, NP, "M" + n, WIN, "ml" + n, 8)
+        Ac = pick_c("A" + o, 0, NP, "M" + n, WIN, "ml" + n, 8, nc, k["ml"], Mc)
+        As = pick_s("A" + o, 0, NP, "M" + n, WIN, "ml" + n, 8, ns, k["ml"], Ms)
         if b == 0:
             send_codes(peers[1], "P1", "A1", 0, NP, "ap1", Ac)
             P = send_scales(peers[1], "P1", "A1", 0, NP, "ap1", As)
+        if b < 2:
+            sent = issued()
+            load("y", "dm" + n, T["cM" + o][:, 0:NP].bitcast(dt.uint8), T["cA" + o][:, 0:NP].bitcast(dt.uint8), Ac, sent)
+            Mc = Ms = load("y", "dm" + n, T["sM" + o][:, 0:NP], T["sA" + o][:, 0:NP], As)
+        if b == 0:
             send_codes(peers[2], "R", "A1", 0, NP, "ar0", Ac)
             ar0 = send_scales(peers[2], "R", "A1", 0, NP, "ar0", As)
-            g.sem_inc(T.sem["gi"], 1)
-            total["gi"] = 2
-            dw[2] = [load("y", "dw2%d" % i, T.wt2[:, 1024 * i:1024 * i + 1024], T.w[:, 4096 + 1024 * i:5120 + 1024 * i], ("gi", 2)) for i in range(2)]
-            dv = load("y", "dv", T.vt[:], T.v[:])
 
     ym = E(lambda q: q.matmul_mx(T.py[:, 0:NP], T.cV[:, 0:NP], T.sV[:, 0:NP], T.cA3[:, 0:NP], T.sA3[:, 0:NP], True, True), qv, Ac, As)
     load("y", "out", T.oc[:, 0:4 * NP], T.cA3[:, 0:NP].bitcast(dt.uint8), Ac)
-    for k in range(4):
-        load("y", "out", T.osc[4 * k:4 * k + 4, 0:NP], T.sA3[32 * k:32 * k + 4, 0:NP], As)
-    yt = V(lambda q: q.tensor_copy(T.yt[:], T.py[:, 0:NP]), ym)
-    load("y", "out", T.y[:], T.yt[:], yt)
-    e = V(lambda q: q.tensor_copy(T.un[:, 4:8], T.ql[:]), ai2)
-    ex = [S(lambda q: q.activation(T.ex[:, NP + 32 * m:NP + 32 * m + 32], T.zb[:, 0:32], F.Identity, bias=T.un[:, 4 + m:5 + m]), e)
-          for m in range(4)][-1]
-    idp = V(lambda q: q.transpose(T.iw2[:, 0:NP], T.ex[:, NP:2 * NP]), ex)
-    kp = [S(lambda q: q.activation(T.kj[:, CAPP * b:CAPP * b + CAPP], T.cw[:, 0:WIN].indirect(T["lz%d" % b][:, 0:3]), F.Copy,
-                                   accum_out=T.kk[:, b:b + 1]), c1, c2, az[b]) for b in range(L)]
-    idn = pick_n(T.im2[:, NP:WIN], "iw2", WIN, "lz2", 3, idp, idw, az[2])
-    idf = pick_n(T.idf[:], "im2", WIN, "ml2", 8, idn, ids, ml)
+    for j in range(4):
+        load("y", "out", T.osc[4 * j:4 * j + 4, 0:NP], T.sA3[32 * j:32 * j + 4, 0:NP], As)
     kk = [V(lambda q: q.tensor_scalar(T.kk[:, 4 + b:5 + b], T.kk[:, b:b + 1], NP - 1.0, T["cc%d" % b][:, NP - 1:NP], A.add, A.min), kp[b], ccs[b])
           for b in range(L)][-1]
     kk = V(lambda q: q.tensor_scalar(T.kk[:, 8:8 + L], T.kk[:, 4:4 + L], 1.0 - NP, None, A.add), kk)
+    yt = V(lambda q: q.tensor_copy(T.yt[:], T.py[:, 0:NP]), ym)
+    load("y", "out", T.y[:], T.yt[:], yt)
     load("y", "out", T.ks[:], T.kk[0:1, 8:8 + L], kk)
+    e = V(lambda q: q.tensor_copy(T.ex[:, NP:2 * NP:32], T.ql[:]), ai2, zx)
+    idp = V(lambda q: q.transpose(T.iw2[:, 0:NP], T.ex[:, NP:2 * NP]), e)
+    idn = pick_n(T.im2[:, NP:WIN], "iw2", WIN, "lz2", 3, idp, idw, az[2])
+    idf = pick_n(T.idf[:], "im2", WIN, "ml2", 8, idn, ids, k["ml"])
     load("y", "out", T.ids[:], T.idf[0:1, :], idf)
 
     for s in sorted(total):

@@ -5,6 +5,7 @@ WIN = NP + CAPP
 A = AluOpType
 F = ActivationFunctionType
 LOADS = {"x": [(0, 0, 2), (0, 2, 2), (1, 0, 4), (L, 0, 0)], "p0": [(2, 0, 4)]}
+ORDER = ("eeomoeooomgoemgmmmnnmn", "eeeeosmosomosmnosmmomnmonmvm", "eteeotoelmtlotolmomnmtomtmonmn")
 
 SCRATCH = {}
 
@@ -220,10 +221,12 @@ def rank_program(g, core, T, topo):
     k = {"wa": None, "wd": None, "ml": None}
     casts, az, ccs, kp = [None] * 4, [], [], []
 
-    def turns(*chains):
-        chains = list(chains)
-        while chains:
-            chains = [c for c in chains if next(c, 0)]
+    def turns(order, **chains):
+        for c in order:
+            next(chains[c], 0)
+        for c in chains:
+            for _ in chains[c]:
+                pass
 
     def count(b):
         kp.append(S(lambda q: q.activation(T.kj[:, CAPP * b:CAPP * b + CAPP], T.cw[:, 0:WIN].indirect(T["lz%d" % b][:, 0:3]), F.Copy,
@@ -232,7 +235,21 @@ def rank_program(g, core, T, topo):
     def expert(b):
         for i in range(4):
             d = [t for (j, w), t in dw[b].items() if j <= i < j + w]
-            k["qw%d" % b] = quant("W%d" % b, 128 * i, 128 * i + 128, T["wt%d" % b][:, 512 * i:512 * i + 512], *d)
+            t = quant("W%d" % b, 128 * i, 128 * i + 128, T["wt%d" % b][:, 512 * i:512 * i + 512], *d)
+            if i == 3:
+                k["qw%d" % b] = t
+            yield 1
+
+    def side_v():
+        k["qv"] = quant("V", 0, NP, T.vt[:], *dw[L].values())
+        yield 1
+
+    def gauges():
+        for j in (1, 2):
+            gg[j] = gauge(j)
+        yield 1
+        qg[1] = quant("G1", 0, NP, T.gt1[:], gg[1])
+        yield 1
 
     def own_list(b):
         n = "%d" % b
@@ -265,7 +282,6 @@ def rank_program(g, core, T, topo):
         sm, cc = T["sm" + n], T["cc" + n]
         k["wd"] = V(lambda q: q.tensor_tensor(T["wd" + n][:], T.ps[:, 0:NP], T.th[:], A.is_lt), k["sc"], th)
         yield 1
-        yield 1
         t = V(lambda q: q.tensor_tensor(T["yd" + n][:], T["wd" + n][:], cc[:], A.mult), k["wd"], k["ct"])
         yield 1
         t = V(lambda q: q.tensor_tensor_scan(T["dd" + n][:], T.rm[:], T["yd" + n][:], 0.0, A.mult, A.add), t, rm)
@@ -289,8 +305,6 @@ def rank_program(g, core, T, topo):
 
     def send_numbers():
         base = float(NP * (rank & ~1))
-        for _ in range(5):
-            yield 1
         t = V(lambda q: q.transpose(T.it[:, 0:NP], T.im1[:, 0:NP]), ids)
         yield 1
         t = V(lambda q: q.tensor_scalar(T.pa[:, 0:2], T.it[:, 0:64:32], 256.0, -257.0 * base, A.mult, A.add), t)
@@ -303,8 +317,6 @@ def rank_program(g, core, T, topo):
 
     def take_numbers():
         base = float(NP * ((rank ^ 2) & ~1))
-        yield 1
-        yield 1
         e = V(lambda q: q.tensor_copy(T.ui[:, 0:2], T.pl[:, 0:2]), k["ai1"])
         yield 1
         e1 = V(lambda q: q.tensor_scalar(T.uj[:, 0:2], T.ui[:, 0:2], 8, None, A.logical_shift_right), e)
@@ -313,12 +325,17 @@ def rank_program(g, core, T, topo):
         e1 = V(lambda q: q.tensor_scalar(T.ex[:, 0:64:32], T.uj[:, 0:2], base, None, A.add), e1, zx)
         e2 = V(lambda q: q.tensor_scalar(T.ex[:, 64:128:32], T.uj[:, 4:6], base, None, A.add), e2)
         yield 1
-        k["idp"] = V(lambda q: q.transpose(T.iw1[:, 0:NP], T.ex[:, 0:NP]), e1, e2)
+        idp = V(lambda q: q.transpose(T.iw1[:, 0:NP], T.ex[:, 0:NP]), e1, e2)
+        idn = pick_n(T.im1[:, NP:WIN], "iw1", WIN, "lz1", 3, idp, idw, az[1])
+        k["ids"] = pick_n(T.im2[:, 0:NP], "im1", WIN, "ml1", 8, idn, ids, old)
+        yield 1
+        e = V(lambda q: q.transpose(T.it[:, NP:2 * NP], T.im2[:, 0:NP]), k["ids"])
+        yield 1
+        e = V(lambda q: q.tensor_copy(T.qx[:], T.it[:, NP:2 * NP:32]), e)
+        k["ai2"] = send(peers[2], T.ql[:], T.qx[:], "ai2", e)
         yield 1
 
     def take_list():
-        for _ in range(3):
-            yield 1
         e = V(lambda q: q.tensor_copy(T.ui[:, 4:8], T.mxl[:]), k["aml"])
         yield 1
         e1 = V(lambda q: q.tensor_scalar(T.uj[:, 8:12], T.ui[:, 4:8], 8, None, A.logical_shift_right), e)
@@ -328,55 +345,48 @@ def rank_program(g, core, T, topo):
         k["pm"] = V(lambda q: q.tensor_copy(T.pm[:, 4:8], T.uj[:, 12:16]), e2)
         yield 1
 
+    def new_columns(b):
+        n = "%d" % b
+        h = T["ht" + n]
+        Pd = (P,)
+        if b == 2:
+            Pd = (pick_c("P2", 0, NP, "R", WIN, "pm", 8, k["pm"], ar0, ar1), pick_s("P2", 0, NP, "R", WIN, "pm", 8, k["pm"], ar0, ar1))
+        mm = [E(lambda q: q.matmul_mx(T.pe[:, 512 * i:512 * i + NP], T["cW" + n][:, 128 * i:128 * i + 128], T["sW" + n][:, 128 * i:128 * i + 128],
+                                      T["cP" + n][:, 0:NP], T["sP" + n][:, 0:NP], True, True), k["qw" + n], casts[i], *Pd) for i in range(4)]
+        for i in range(3):
+            casts[i] = S(lambda q: q.activation(h[:, i:512:4], T.pe[:, 512 * i:512 * i + NP], F.Copy, scale=0.0625), mm[i])
+        yield 1
+        casts[3] = V(lambda q: q.tensor_scalar(h[:, 3:512:4], T.pe[:, 1536:1536 + NP], 0.0625, None, A.mult), mm[3])
+        yield 1
+        k["qn"] = quant("X" + n, 0, NP, h[:], *casts)
+        yield 1
+
     for b in range(L):
         n = "%d" % b
         if b == 1:
             ids = pick_n(T.im1[:, 0:NP], "im0", WIN, "ml0", 8, idn, ids, k["ml"])
         k["sc"] = E(lambda q: q.matmul_mx(T.ps[:, 0:NP], T["cG" + n][:, 0:NP], T["sG" + n][:, 0:NP], T["cA" + n][:, 0:NP],
                                           T["sA" + n][:, 0:NP], True, True), qg[b], Ac, As, k["wa"], k["wd"])
-        Pd, old = (P,), k["ml"]
+        old = k["ml"]
         if b == 0:
-            turns(own_list(0), merging_list(0))
+            turns(ORDER[0], o=own_list(0), m=merging_list(0), g=gauges(), e=expert(0), n=new_columns(0))
             point("p0", P)
+            qg[2] = quant("G2", 0, NP, T.gt2[:], gg[2])
         if b == 1:
-            turns(own_list(1), merging_list(1), send_numbers())
+            turns(ORDER[1], e=expert(1), o=own_list(1), s=send_numbers(), m=merging_list(1), n=new_columns(1), v=side_v())
+            last = expert(2)
+            next(last)
         if b == 2:
-            expert(2)
-            turns(own_list(2), take_numbers(), take_list(), merging_list(2))
-        if b < 2:
-            idw = pick_n(T["iw" + n][:, NP:WIN], "im" + n, NP, "lo" + n, 3, k["lo"], ids)
-        if b == 0:
-            for j in (1, 2):
-                gg[j] = gauge(j)
-            expert(0)
-            for j in (1, 2):
-                qg[j] = quant("G%d" % j, 0, NP, T["gt%d" % j][:], gg[j])
-        if b == 2:
-            Pd = (pick_c("P2", 0, NP, "R", WIN, "pm", 8, k["pm"], ar0, ar1), pick_s("P2", 0, NP, "R", WIN, "pm", 8, k["pm"], ar0, ar1))
-            idn = pick_n(T.im1[:, NP:WIN], "iw1", WIN, "lz1", 3, k["idp"], idw, az[1])
-            ids = pick_n(T.im2[:, 0:NP], "im1", WIN, "ml1", 8, idn, ids, old)
-            e = V(lambda q: q.transpose(T.it[:, NP:2 * NP], T.im2[:, 0:NP]), ids)
-            e = V(lambda q: q.tensor_copy(T.qx[:], T.it[:, NP:2 * NP:32]), e)
-            ai2 = send(peers[2], T.ql[:], T.qx[:], "ai2", e)
-        h = T["ht" + n]
-        mm = [E(lambda q: q.matmul_mx(T.pe[:, 512 * i:512 * i + NP], T["cW" + n][:, 128 * i:128 * i + 128], T["sW" + n][:, 128 * i:128 * i + 128],
-                                      T["cP" + n][:, 0:NP], T["sP" + n][:, 0:NP], True, True), k["qw" + n], casts[i], *Pd) for i in range(4)]
-        for i in range(3):
-            casts[i] = S(lambda q: q.activation(h[:, i:512:4], T.pe[:, 512 * i:512 * i + NP], F.Copy, scale=0.0625), mm[i])
-        if b == 0:
-            expert(1)
-        casts[3] = V(lambda q: q.tensor_scalar(h[:, 3:512:4], T.pe[:, 1536:1536 + NP], 0.0625, None, A.mult), mm[3])
-        qn = quant("X" + n, 0, NP, h[:], *casts)
+            turns(ORDER[2], e=last, t=take_numbers(), o=own_list(2), l=take_list(), n=new_columns(2), m=merging_list(2))
+            ids, ai2 = k["ids"], k["ai2"]
+        idw = pick_n(T["iw" + n][:, NP:WIN], "im" + n, NP, "lo" + n, 3, k["lo"], ids)
         if b == 0:
             idn = pick_n(T.im0[:, NP:WIN], "iw0", WIN, "lz0", 3, idp, idw, az[0])
-        if b == 1:
-            qv = quant("V", 0, NP, T.vt[:], *dw[L].values())
         if b == 2:
-            idw = pick_n(T.iw2[:, NP:WIN], "im2", NP, "lo2", 3, k["lo"], ids)
             for j in range(L):
                 count(j)
-        nc = pick_c("M" + n, NP, WIN, "X" + n, WIN, "lz" + n, 3, qn, k["xc"], az[b])
-        ns = pick_s("M" + n, NP, WIN, "X" + n, WIN, "lz" + n, 3, qn, k["xs"], az[b])
+        nc = pick_c("M" + n, NP, WIN, "X" + n, WIN, "lz" + n, 3, k["qn"], k["xc"], az[b])
+        ns = pick_s("M" + n, NP, WIN, "X" + n, WIN, "lz" + n, 3, k["qn"], k["xs"], az[b])
         if b == 1:
             send_codes(peers[2], "R", "M1", NP, WIN, "ar1", nc)
             ar1 = send_scales(peers[2], "R", "M1", NP, WIN, "ar1", ns)
@@ -394,18 +404,18 @@ def rank_program(g, core, T, topo):
             send_codes(peers[2], "R", "A1", 0, NP, "ar0", Ac)
             ar0 = send_scales(peers[2], "R", "A1", 0, NP, "ar0", As)
 
-    ym = E(lambda q: q.matmul_mx(T.py[:, 0:NP], T.cV[:, 0:NP], T.sV[:, 0:NP], T.cA3[:, 0:NP], T.sA3[:, 0:NP], True, True), qv, Ac, As)
+    ym = E(lambda q: q.matmul_mx(T.py[:, 0:NP], T.cV[:, 0:NP], T.sV[:, 0:NP], T.cA3[:, 0:NP], T.sA3[:, 0:NP], True, True), k["qv"], Ac, As)
     load("y", "out", T.oc[:, 0:4 * NP], T.cA3[:, 0:NP].bitcast(dt.uint8), Ac)
     for j in range(4):
         load("y", "out", T.osc[4 * j:4 * j + 4, 0:NP], T.sA3[32 * j:32 * j + 4, 0:NP], As)
     kk = [V(lambda q: q.tensor_scalar(T.kk[:, 4 + b:5 + b], T.kk[:, b:b + 1], NP - 1.0, T["cc%d" % b][:, NP - 1:NP], A.add, A.min), kp[b], ccs[b])
           for b in range(L)][-1]
+    e = V(lambda q: q.tensor_copy(T.ex[:, NP:2 * NP:32], T.ql[:]), ai2, zx)
     kk = V(lambda q: q.tensor_scalar(T.kk[:, 8:8 + L], T.kk[:, 4:4 + L], 1.0 - NP, None, A.add), kk)
+    idp = V(lambda q: q.transpose(T.iw2[:, 0:NP], T.ex[:, NP:2 * NP]), e)
     yt = V(lambda q: q.tensor_copy(T.yt[:], T.py[:, 0:NP]), ym)
     load("y", "out", T.y[:], T.yt[:], yt)
     load("y", "out", T.ks[:], T.kk[0:1, 8:8 + L], kk)
-    e = V(lambda q: q.tensor_copy(T.ex[:, NP:2 * NP:32], T.ql[:]), ai2, zx)
-    idp = V(lambda q: q.transpose(T.iw2[:, 0:NP], T.ex[:, NP:2 * NP]), e)
     idn = pick_n(T.im2[:, NP:WIN], "iw2", WIN, "lz2", 3, idp, idw, az[2])
     idf = pick_n(T.idf[:], "im2", WIN, "ml2", 8, idn, ids, k["ml"])
     load("y", "out", T.ids[:], T.idf[0:1, :], idf)

from concourse.mybir import dt, AluOpType, ActivationFunctionType

L, CAPP, NP = 3, 48, 128
WIN = NP + CAPP
A = AluOpType
F = ActivationFunctionType
LOADS = {"x": [(0, 0, 2), (0, 2, 2), (1, 0, 4), (L, 0, 0)], "p0": [(2, 0, 4)]}
ORDER = ("eeomoeooomgoemgmmmnnmn", "eeeeosmosomosmnosmmomnmonmvm", "eteeotoelmtlotolmomnmtomtmonmn")

SCRATCH = {}


def _mx(name, n):
    SCRATCH["c" + name] = ("sbuf", [128, n], "float8_e4m3fn_x4")
    SCRATCH["s" + name] = ("sbuf", [128, n], "uint8")


def _sb(name, n, dtype="float32"):
    SCRATCH[name] = ("sbuf", [128, n], dtype)


for _b in range(L):
    _mx("A%d" % _b, 128)
    _mx("M%d" % _b, WIN)
    _mx("X%d" % _b, WIN)
    _mx("G%d" % _b, 128)
    _mx("W%d" % _b, 512)
    _sb("wt%d" % _b, 2048, "bfloat16")
    _sb("gt%d" % _b, 512, "bfloat16")
    _sb("ht%d" % _b, 512, "bfloat16")
    _sb("wa%d" % _b, 128, "bfloat16")
    _sb("cc%d" % _b, 128, "bfloat16")
    _sb("wd%d" % _b, 128, "bfloat16")
    _sb("yd%d" % _b, 128, "bfloat16")
    _sb("dd%d" % _b, 128, "bfloat16")
    _sb("jk%d" % _b, 384, "bfloat16")
    _sb("su%d" % _b, 4)
    _sb("sm%d" % _b, 64)
    _sb("zz%d" % _b, 4, "uint16")
    _sb("lo%d" % _b, 4, "uint16")
    _sb("ml%d" % _b, 8, "uint16")
    _sb("lz%d" % _b, 4, "uint16")
    _sb("im%d" % _b, WIN)
    _sb("iw%d" % _b, WIN)
_mx("A3", 128)
_mx("P0", 128)
_mx("P1", 128)
_mx("R", WIN)
_mx("P2", 128)
_mx("V", 128)
_sb("xt", 512, "bfloat16")
_sb("ut", 4 * L, "bfloat16")
_sb("vt", 512, "bfloat16")
_sb("zb", 128, "bfloat16")
_sb("ia", 128, "int32")
_sb("ib", 128, "int32")
_sb("iq", 8, "int32")
_sb("ir", 8, "int32")
_sb("ic", 8)
_sb("pj", 24)
_sb("th", 128)
_sb("r0", 128, "bfloat16")
_sb("rm", 128, "bfloat16")
_sb("cw", WIN)
_sb("kj", CAPP * L)
_sb("it", 256)
_sb("pa", 8)
_sb("px", 4, "uint16")
_sb("pl", 4, "uint16")
_sb("qx", 4, "uint16")
_sb("ql", 4, "uint16")
_sb("mx1", 4, "uint16")
_sb("mxl", 4, "uint16")
_sb("pm", 8, "uint16")
_sb("ui", 16, "int32")
_sb("uj", 16, "int32")
_sb("ex", 256)
_sb("idf", 128)
_sb("kk", 12)
_sb("yt", 128)
SCRATCH["pe"] = ("psum", [128, 2048], "float32")
SCRATCH["ps"] = ("psum", [128, 512], "float32")
SCRATCH["py"] = ("psum", [128, 512], "float32")

SEMAPHORES = (["vs", "ss", "ts", "gs", "gi", "sent", "dx", "du", "dv", "out", "dm0", "dm1"]
              + ["dw%d%d" % (b, i) for b in range(L) for i in range(4)]
              + ["ap0", "ap1", "ar0", "ar1", "az0", "az1", "az2", "ai1", "ai2", "aml"])


def rank_program(g, core, T, topo):
    rank = T.rank_of(core)
    if rank is None:
        return
    peers = [T.cores[rank ^ (1 << b)] for b in range(L)]
    queue = {"v": g.vector, "s": g.scalar, "t": g.tensor, "g": g, "y": g.sync}
    total, known = {}, {q: {} for q in queue}

    def need(q, deps):
        for d in deps:
            if d is None:
                continue
            s, n = d
            if known[q].get(s, 0) < n:
                queue[q].wait_ge(T.sem[s], n)
                known[q][s] = n

    def did(instr, s, n):
        instr.then_inc(T.sem[s], n)
        total[s] = total.get(s, 0) + n
        return (s, total[s])

    def V(call, *deps):
        need("v", deps)
        return did(call(g.vector), "vs", 1)

    def S(call, *deps):
        need("s", deps)
        return did(call(g.scalar), "ss", 1)

    def E(call, *deps):
        need("t", deps)
        return did(call(g.tensor), "ts", 1)

    def I(call, *deps):
        need("g", deps)
        return did(call(g), "gs", 1)

    def load(q, sem, out, in_, *deps):
        need(q, deps)
        return did(queue[q].dma_start(out, in_), sem, 16)

    def mask(dst, quiet=False):
        es = topo.engines(core, dst)
        if quiet:
            es = [e for e in es if e not in topo.engines(core, peers[2])] or es
        m = 0
        for e in es:
            m |= 1 << e
        return m, len(es)

    def send(dst, out, in_, sem, *deps, quiet=False):
        need("g", deps)
        m, n = mask(dst, quiet)
        rid, pid, _ = topo.addr(dst)
        g.remote_dma(out, in_, T.sem[sem], T.sem["sent"], pid, rid, m)
        total["sent"] = total.get("sent", 0) + n
        total[sem] = total.get(sem, 0) + n
        return (sem, total[sem])

    def send_codes(dst, to, frm, a, b, sem, *deps):
        return send(dst, T["c" + to][:, a:b].bitcast(dt.uint8), T["c" + frm][:, a:b].bitcast(dt.uint8), sem, *deps)

    def send_scales(dst, to, frm, a, b, sem, *deps):
        return send(dst, T["s" + to][:, a:b], T["s" + frm][:, a:b], sem, *deps)

    def pick_c(to, a, b, frm, n, off, k, *deps):
        return V(lambda q: q.tensor_copy(T["c" + to][:, a:b].bitcast(dt.uint32),
                                         T["c" + frm][:, 0:n].bitcast(dt.uint32).indirect(T[off][:, 0:k])), *deps)

    def pick_s(to, a, b, frm, n, off, k, *deps):
        return S(lambda q: q.activation(T["s" + to][:, a:b], T["s" + frm][:, 0:n].indirect(T[off][:, 0:k]), F.Copy), *deps)

    def pick_n(out, frm, n, off, k, *deps):
        return S(lambda q: q.activation(out, T[frm][:, 0:n].indirect(T[off][:, 0:k]), F.Copy), *deps)

    def quant(to, a, b, in_, *deps):
        return V(lambda q: q.quantize_mx(T["c" + to][:, a:b], T["s" + to][:, a:b], in_), *deps)

    dx = load("y", "dx", T.xt[:], T.x[:])
    du = load("s", "du", T.ut[:], T.u[:, 0:4 * L])
    dw = {b: {} for b in range(L + 1)}

    def issued():
        g.sem_inc(T.sem["gi"], 1)
        total["gi"] = total.get("gi", 0) + 1
        return ("gi", total["gi"])

    def point(name, *deps):
        for b, i, w in LOADS[name]:
            if b == L:
                dw[b][i, w] = load("y", "dv", T.vt[:], T.v[:], *deps)
            else:
                dw[b][i, w] = load("y", "dw%d%d" % (b, i), T["wt%d" % b][:, 512 * i:512 * i + 512 * w],
                                   T.w[:, 2048 * b + 512 * i:2048 * b + 512 * i + 512 * w], *deps)

    point("x")

    zb = V(lambda q: q.memset(T.zb[:], 0.0))
    zx = V(lambda q: q.memset(T.ex[:], 0.0))
    c1 = V(lambda q: q.memset(T.cw[:, 0:NP], 1.0))
    c2 = V(lambda q: q.memset(T.cw[:, NP:WIN], 0.0))
    flag = {"allow_small_or_imprecise_dtypes": True}
    iq = I(lambda q: q.iota(T.iq[:], [[0, 8]], 0, 1))
    ic = I(lambda q: q.iota(T.ic[:], [[16, 8]], 0, 0, **flag))
    ia = I(lambda q: q.iota(T.ia[:], [[1, 128]], 128, -1))
    r0 = I(lambda q: q.iota(T.r0[:], [[0, 8], [1, 16]], 0, 0, **flag))
    im = I(lambda q: q.iota(T.im0[:, 0:NP], [[1, NP]], rank * NP, 0, **flag))
    iw = I(lambda q: q.iota(T.iw0[:, 0:NP], [[1, NP]], (rank ^ 1) * NP, 0, **flag))
    p8, jb, jc = T.pj[:, 0:8], T.pj[:, 8:16], T.pj[:, 16:24]
    ir = V(lambda q: q.tensor_scalar(T["ir"][:], T.iq[:], 15, None, A.bitwise_and), iq)
    kp8 = V(lambda q: q.tensor_tensor(p8, T["ir"][:], T.ic[:], A.add), ir, ic)
    kjb = V(lambda q: q.tensor_scalar(jb, p8, NP - 0.5, None, A.add), kp8)
    kjc = V(lambda q: q.tensor_scalar(jc, p8, NP - 1.0, None, A.add), kp8)
    ib = V(lambda q: q.tensor_scalar(T.ib[:], T.ia[:], 15, None, A.bitwise_and), ia)
    th = V(lambda q: q.tensor_scalar(T.th[:], T.ib[:], 0.0, -1e29, A.not_equal, A.mult), ib)
    rm = V(lambda q: q.tensor_scalar(T.rm[:], T.r0[:], 0.0, None, A.is_gt), r0)

    def gauge(b):
        return [S(lambda q: q.activation(T["gt%d" % b][:, t:512:4], T.zb[:], F.Identity, bias=T.ut[:, 4 * b + t:4 * b + t + 1]), zb, du)
                for t in range(4)][-1]

    gg = {0: gauge(0)}
    Ac = As = quant("A0", 0, NP, T.xt[:], dx)
    qg = {0: quant("G0", 0, NP, T.gt0[:], gg[0])}
    Mc = Ms = quant("M0", 0, NP, T.xt[:], dx)

    send_codes(peers[0], "P0", "A0", 0, NP, "ap0", Ac)
    P = send_scales(peers[0], "P0", "A0", 0, NP, "ap0", As)

    ids, idp = im, iw
    k = {"wa": None, "wd": None, "ml": None}
    casts, az, ccs, kp = [None] * 4, [], [], []

    def turns(order, **chains):
        for c in order:
            next(chains[c], 0)
        for c in chains:
            for _ in chains[c]:
                pass

    def count(b):
        kp.append(S(lambda q: q.activation(T.kj[:, CAPP * b:CAPP * b + CAPP], T.cw[:, 0:WIN].indirect(T["lz%d" % b][:, 0:3]), F.Copy,
                                           accum_out=T.kk[:, b:b + 1]), c1, c2, az[b]))

    def expert(b):
        for i in range(4):
            d = [t for (j, w), t in dw[b].items() if j <= i < j + w]
            t = quant("W%d" % b, 128 * i, 128 * i + 128, T["wt%d" % b][:, 512 * i:512 * i + 512], *d)
            if i == 3:
                k["qw%d" % b] = t
            yield 1

    def side_v():
        k["qv"] = quant("V", 0, NP, T.vt[:], *dw[L].values())
        yield 1

    def gauges():
        for j in (1, 2):
            gg[j] = gauge(j)
        yield 1
        qg[1] = quant("G1", 0, NP, T.gt1[:], gg[1])
        yield 1

    def own_list(b):
        n = "%d" % b
        sm, su, cc = T["sm" + n], T["su" + n], T["cc" + n]
        k["wa"] = V(lambda q: q.tensor_scalar(T["wa" + n][:], T.ps[:, 0:NP], 0.0, None, A.is_lt), k["sc"])
        yield 1
        k["ct"] = V(lambda q: q.tensor_tensor_scan(cc[:], T["wa" + n][:], T["wa" + n][:], NP - 1.0, A.add, A.max), k["wa"])
        ccs.append(k["ct"])
        sums = [S(lambda q: q.activation(T["jk" + n][:, NP * c:NP * c + NP], cc[:], F.Sign, bias=T.pj[:, 8 + c:9 + c], scale=-1.0,
                                         accum_out=su[:, c:c + 1]), k["ct"], kjb) for c in range(3)]
        yield 1
        for c in range(3):
            t = V(lambda q: q.tensor_scalar(sm[:, c:c + 1], cc[:, NP - 1:NP], T.pj[:, 16 + c:17 + c], T.pj[:, c:c + 1], A.is_le, A.mult),
                  k["ct"], kjc)
        yield 1
        t = V(lambda q: q.tensor_scalar(sm[:, 8:11], sm[:, 0:3], 64.0, None, A.add), t)
        yield 1
        for c in range(3):
            z = V(lambda q: q.tensor_scalar(T["zz" + n][:, c:c + 1], su[:, c:c + 1], 0.5, sm[:, 8 + c:9 + c], A.mult, A.add), t, sums[c])
        az.append(send(peers[b], T["lz" + n][:, 0:3], T["zz" + n][:, 0:3], "az" + n, z, quiet=(b == 1)))
        yield 1
        lo = k["lo"] = V(lambda q: q.tensor_scalar(T["lo" + n][:, 0:3], T["zz" + n][:, 0:3], float(NP - 1), None, A.min), z)
        yield 1
        k["xc"] = pick_c("X" + n, NP, WIN, "A" + n, NP, "lo" + n, 3, lo, Ac)
        k["xs"] = pick_s("X" + n, NP, WIN, "A" + n, NP, "lo" + n, 3, lo, As)
        yield 1

    def merging_list(b):
        n = "%d" % b
        sm, cc = T["sm" + n], T["cc" + n]
        k["wd"] = V(lambda q: q.tensor_tensor(T["wd" + n][:], T.ps[:, 0:NP], T.th[:], A.is_lt), k["sc"], th)
        yield 1
        t = V(lambda q: q.tensor_tensor(T["yd" + n][:], T["wd" + n][:], cc[:], A.mult), k["wd"], k["ct"])
        yield 1
        t = V(lambda q: q.tensor_tensor_scan(T["dd" + n][:], T.rm[:], T["yd" + n][:], 0.0, A.mult, A.add), t, rm)
        yield 1
        d8 = T["dd" + n][:, 15:128:16]
        t = V(lambda q: q.tensor_scalar(sm[:, 16:24], d8, float(WIN - 1), None, A.is_le), t)
        yield 1
        t = V(lambda q: q.tensor_tensor(sm[:, 24:32], sm[:, 16:24], d8, A.mult), t)
        yield 1
        t = V(lambda q: q.tensor_tensor(sm[:, 32:40], sm[:, 24:32], T.pj[:, 0:8], A.max), t, kp8)
        yield 1
        k["ml"] = V(lambda q: q.tensor_copy(T["ml" + n][:], sm[:, 32:40]), t)
        if b == 1:
            t = V(lambda q: q.tensor_scalar(sm[:, 40:44], sm[:, 32:36], 256.0, None, A.mult), t)
            yield 1
            t = V(lambda q: q.tensor_tensor(sm[:, 44:48], sm[:, 40:44], sm[:, 36:40], A.add), t)
            yield 1
            t = V(lambda q: q.tensor_copy(T.mx1[:], sm[:, 44:48]), t)
            k["aml"] = send(peers[2], T.mxl[:], T.mx1[:], "aml", t)
        yield 1

    def send_numbers():
        base = float(NP * (rank & ~1))
        t = V(lambda q: q.transpose(T.it[:, 0:NP], T.im1[:, 0:NP]), ids)
        yield 1
        t = V(lambda q: q.tensor_scalar(T.pa[:, 0:2], T.it[:, 0:64:32], 256.0, -257.0 * base, A.mult, A.add), t)
        yield 1
        t = V(lambda q: q.tensor_tensor(T.pa[:, 4:6], T.pa[:, 0:2], T.it[:, 64:128:32], A.add), t)
        yield 1
        t = V(lambda q: q.tensor_copy(T.px[:, 0:2], T.pa[:, 4:6]), t)
        k["ai1"] = send(peers[1], T.pl[:, 0:2], T.px[:, 0:2], "ai1", t, quiet=True)
        yield 1

    def take_numbers():
        base = float(NP * ((rank ^ 2) & ~1))
        e = V(lambda q: q.tensor_copy(T.ui[:, 0:2], T.pl[:, 0:2]), k["ai1"])
        yield 1
        e1 = V(lambda q: q.tensor_scalar(T.uj[:, 0:2], T.ui[:, 0:2], 8, None, A.logical_shift_right), e)
        e2 = V(lambda q: q.tensor_scalar(T.uj[:, 4:6], T.ui[:, 0:2], 255, None, A.bitwise_and), e)
        yield 1
        e1 = V(lambda q: q.tensor_scalar(T.ex[:, 0:64:32], T.uj[:, 0:2], base, None, A.add), e1, zx)
        e2 = V(lambda q: q.tensor_scalar(T.ex[:, 64:128:32], T.uj[:, 4:6], base, None, A.add), e2)
        yield 1
        idp = V(lambda q: q.transpose(T.iw1[:, 0:NP], T.ex[:, 0:NP]), e1, e2)
        idn = pick_n(T.im1[:, NP:WIN], "iw1", WIN, "lz1", 3, idp, idw, az[1])
        k["ids"] = pick_n(T.im2[:, 0:NP], "im1", WIN, "ml1", 8, idn, ids, old)
        yield 1
        e = V(lambda q: q.transpose(T.it[:, NP:2 * NP], T.im2[:, 0:NP]), k["ids"])
        yield 1
        e = V(lambda q: q.tensor_copy(T.qx[:], T.it[:, NP:2 * NP:32]), e)
        k["ai2"] = send(peers[2], T.ql[:], T.qx[:], "ai2", e)
        yield 1

    def take_list():
        e = V(lambda q: q.tensor_copy(T.ui[:, 4:8], T.mxl[:]), k["aml"])
        yield 1
        e1 = V(lambda q: q.tensor_scalar(T.uj[:, 8:12], T.ui[:, 4:8], 8, None, A.logical_shift_right), e)
        e2 = V(lambda q: q.tensor_scalar(T.uj[:, 12:16], T.ui[:, 4:8], 255, None, A.bitwise_and), e)
        yield 1
        e1 = V(lambda q: q.tensor_copy(T.pm[:, 0:4], T.uj[:, 8:12]), e1)
        k["pm"] = V(lambda q: q.tensor_copy(T.pm[:, 4:8], T.uj[:, 12:16]), e2)
        yield 1

    def new_columns(b):
        n = "%d" % b
        h = T["ht" + n]
        Pd = (P,)
        if b == 2:
            Pd = (pick_c("P2", 0, NP, "R", WIN, "pm", 8, k["pm"], ar0, ar1), pick_s("P2", 0, NP, "R", WIN, "pm", 8, k["pm"], ar0, ar1))
        mm = [E(lambda q: q.matmul_mx(T.pe[:, 512 * i:512 * i + NP], T["cW" + n][:, 128 * i:128 * i + 128], T["sW" + n][:, 128 * i:128 * i + 128],
                                      T["cP" + n][:, 0:NP], T["sP" + n][:, 0:NP], True, True), k["qw" + n], casts[i], *Pd) for i in range(4)]
        for i in range(3):
            casts[i] = S(lambda q: q.activation(h[:, i:512:4], T.pe[:, 512 * i:512 * i + NP], F.Copy, scale=0.0625), mm[i])
        yield 1
        casts[3] = V(lambda q: q.tensor_scalar(h[:, 3:512:4], T.pe[:, 1536:1536 + NP], 0.0625, None, A.mult), mm[3])
        yield 1
        k["qn"] = quant("X" + n, 0, NP, h[:], *casts)
        yield 1

    for b in range(L):
        n = "%d" % b
        if b == 1:
            ids = pick_n(T.im1[:, 0:NP], "im0", WIN, "ml0", 8, idn, ids, k["ml"])
        k["sc"] = E(lambda q: q.matmul_mx(T.ps[:, 0:NP], T["cG" + n][:, 0:NP], T["sG" + n][:, 0:NP], T["cA" + n][:, 0:NP],
                                          T["sA" + n][:, 0:NP], True, True), qg[b], Ac, As, k["wa"], k["wd"])
        old = k["ml"]
        if b == 0:
            turns(ORDER[0], o=own_list(0), m=merging_list(0), g=gauges(), e=expert(0), n=new_columns(0))
            point("p0", P)
            qg[2] = quant("G2", 0, NP, T.gt2[:], gg[2])
        if b == 1:
            turns(ORDER[1], e=expert(1), o=own_list(1), s=send_numbers(), m=merging_list(1), n=new_columns(1), v=side_v())
            last = expert(2)
            next(last)
        if b == 2:
            turns(ORDER[2], e=last, t=take_numbers(), o=own_list(2), l=take_list(), n=new_columns(2), m=merging_list(2))
            ids, ai2 = k["ids"], k["ai2"]
        idw = pick_n(T["iw" + n][:, NP:WIN], "im" + n, NP, "lo" + n, 3, k["lo"], ids)
        if b == 0:
            idn = pick_n(T.im0[:, NP:WIN], "iw0", WIN, "lz0", 3, idp, idw, az[0])
        if b == 2:
            for j in range(L):
                count(j)
        nc = pick_c("M" + n, NP, WIN, "X" + n, WIN, "lz" + n, 3, k["qn"], k["xc"], az[b])
        ns = pick_s("M" + n, NP, WIN, "X" + n, WIN, "lz" + n, 3, k["qn"], k["xs"], az[b])
        if b == 1:
            send_codes(peers[2], "R", "M1", NP, WIN, "ar1", nc)
            ar1 = send_scales(peers[2], "R", "M1", NP, WIN, "ar1", ns)
        o = "%d" % (b + 1)
        Ac = pick_c("A" + o, 0, NP, "M" + n, WIN, "ml" + n, 8, nc, k["ml"], Mc)
        As = pick_s("A" + o, 0, NP, "M" + n, WIN, "ml" + n, 8, ns, k["ml"], Ms)
        if b == 0:
            send_codes(peers[1], "P1", "A1", 0, NP, "ap1", Ac)
            P = send_scales(peers[1], "P1", "A1", 0, NP, "ap1", As)
        if b < 2:
            sent = issued()
            load("y", "dm" + n, T["cM" + o][:, 0:NP].bitcast(dt.uint8), T["cA" + o][:, 0:NP].bitcast(dt.uint8), Ac, sent)
            Mc = Ms = load("y", "dm" + n, T["sM" + o][:, 0:NP], T["sA" + o][:, 0:NP], As)
        if b == 0:
            send_codes(peers[2], "R", "A1", 0, NP, "ar0", Ac)
            ar0 = send_scales(peers[2], "R", "A1", 0, NP, "ar0", As)

    ym = E(lambda q: q.matmul_mx(T.py[:, 0:NP], T.cV[:, 0:NP], T.sV[:, 0:NP], T.cA3[:, 0:NP], T.sA3[:, 0:NP], True, True), k["qv"], Ac, As)
    load("y", "out", T.oc[:, 0:4 * NP], T.cA3[:, 0:NP].bitcast(dt.uint8), Ac)
    for j in range(4):
        load("y", "out", T.osc[4 * j:4 * j + 4, 0:NP], T.sA3[32 * j:32 * j + 4, 0:NP], As)
    kk = [V(lambda q: q.tensor_scalar(T.kk[:, 4 + b:5 + b], T.kk[:, b:b + 1], NP - 1.0, T["cc%d" % b][:, NP - 1:NP], A.add, A.min), kp[b], ccs[b])
          for b in range(L)][-1]
    e = V(lambda q: q.tensor_copy(T.ex[:, NP:2 * NP:32], T.ql[:]), ai2, zx)
    kk = V(lambda q: q.tensor_scalar(T.kk[:, 8:8 + L], T.kk[:, 4:4 + L], 1.0 - NP, None, A.add), kk)
    idp = V(lambda q: q.transpose(T.iw2[:, 0:NP], T.ex[:, NP:2 * NP]), e)
    yt = V(lambda q: q.tensor_copy(T.yt[:], T.py[:, 0:NP]), ym)
    load("y", "out", T.y[:], T.yt[:], yt)
    load("y", "out", T.ks[:], T.kk[0:1, 8:8 + L], kk)
    idn = pick_n(T.im2[:, NP:WIN], "iw2", WIN, "lz2", 3, idp, idw, az[2])
    idf = pick_n(T.idf[:], "im2", WIN, "ml2", 8, idn, ids, k["ml"])
    load("y", "out", T.ids[:], T.idf[0:1, :], idf)

    for s in sorted(total):
        need("g", [(s, total[s])])
